import numpy as np
import ml_dtypes


def mxq(x, axis, fmt="e4m3"):
    dtype, down = {"e4m3": (ml_dtypes.float8_e4m3fn, 7), "e5m2": (ml_dtypes.float8_e5m2, 14)}[fmt]
    v = np.moveaxis(np.asarray(x, np.float32).astype(ml_dtypes.bfloat16).astype(np.float64), axis, -1)
    blocks = v.reshape(v.shape[:-1] + (-1, 32))
    amax = np.abs(blocks).max(-1, keepdims=True)
    byte = np.maximum(np.where(amax > 0, np.frexp(amax)[1] - 1 + 127, 0) - down, 1)
    scale = np.exp2(byte - 127.0)
    codes = (blocks / scale).astype(np.float32).astype(dtype).astype(np.float64)
    return np.moveaxis((codes * scale).reshape(v.shape), -1, axis)


WIDE = False


def mx_kscale(k):
    if not WIDE:
        return np.ones(k)
    levels = np.array([10, -10, 5, -5, 0])
    if k % 512:
        return np.exp2(np.random.permutation(np.resize(levels, k // 32))).repeat(32)
    a = np.empty((k // 512, 16))
    for p in range(k // 512):
        a[p, :8] = np.random.permutation(np.resize(levels, 8))
        for g in range(8):
            far = levels[np.abs(levels - a[p, g]) >= 10]
            a[p, g + 8] = far[np.random.randint(len(far))]
    return np.exp2(a.ravel()).repeat(32)


def f64(x):
    return np.asarray(x).astype(np.float64)


def striped(idx):
    return np.tile(idx.reshape(-1, 16).T, (8, 1)).astype(np.uint16)


def unstriped(offs):
    return offs[:16].T.reshape(-1).astype(np.int64)


def striped8(idx):
    return np.concatenate([x.reshape(-1, 16).T for x in idx]).astype(np.uint16)


def runs(offs, k):
    lists = np.stack([offs[16 * r : 16 * r + 16].T.reshape(-1) for r in range(8)]).astype(np.int64)
    return lists[np.arange(k) % 512 // 64]


def pack_weight(w):
    k, n = w.shape
    w = f64(np.asarray(w, np.float32).astype(ml_dtypes.bfloat16)).reshape(k // 32, 32, n)
    amax = np.abs(w).max(1)
    byte = np.clip(np.where(amax > 0, np.frexp(amax)[1] - 1 + 127 - 7, 1), 1, 254)
    scaled = (w * np.exp2(127.0 - byte)[:, None, :]).reshape(k, n).astype(np.float32)
    words = np.ascontiguousarray(scaled.reshape(k // 512, 128, 4, n).transpose(0, 1, 3, 2)).astype(ml_dtypes.float8_e4m3fn).view(np.uint8)
    return words, np.ascontiguousarray(byte.astype(np.uint8).reshape(k // 512, 16, n))


def unpack_weight(words, scales):
    g, p, n, _ = words.shape
    vals = np.ascontiguousarray(words).view(ml_dtypes.float8_e4m3fn).astype(np.float64) * np.repeat(np.exp2(scales.astype(np.float64) - 127.0), 8, axis=1)[..., None]
    return vals.transpose(0, 1, 3, 2).reshape(g * 512, n)


E2M1 = np.array([0.0, 0.5, 1.0, 1.5, 2.0, 3.0, 4.0, 6.0, -0.0, -0.5, -1.0, -1.5, -2.0, -3.0, -4.0, -6.0])


def pack_fp4(w):
    k, n = w.shape
    w = f64(np.asarray(w, np.float32).astype(ml_dtypes.bfloat16)).reshape(k // 32, 32, n)
    amax = np.abs(w).max(1)
    mant, ex = np.frexp(amax / 6.0)
    byte = np.clip(np.where(amax > 0, np.where(mant > 0.5, ex, ex - 1) + 127, 1), 1, 254)
    scaled = (w * np.exp2(127.0 - byte)[:, None, :]).reshape(k, n).astype(np.float32)
    c = np.ascontiguousarray(scaled.reshape(k // 512, 128, 4, n).transpose(0, 1, 3, 2)).astype(ml_dtypes.float4_e2m1fn).view(np.uint8) & 0xF
    words = (c[..., 0::2] | (c[..., 1::2] << 4)).reshape(k // 512, 128, 2 * n)
    return np.ascontiguousarray(words), np.ascontiguousarray(byte.astype(np.uint8).reshape(k // 512, 16, n))


def unpack_fp4(words, scales):
    g, _, n = scales.shape
    words = np.ascontiguousarray(words).reshape(g, 128, n, 2)
    nib = np.empty((g, 128, n, 4), np.uint8)
    nib[..., 0::2] = words & 0xF
    nib[..., 1::2] = words >> 4
    vals = E2M1[nib] * np.repeat(np.exp2(scales.astype(np.float64) - 127.0), 8, axis=1)[..., None]
    return vals.transpose(0, 1, 3, 2).reshape(g * 512, n)


def sigmoid(v):
    return 1.0 / (1.0 + np.exp(-np.maximum(v, -700.0)))

def planes(y):
    n, m = y.shape
    v = y.astype(np.float32).astype(ml_dtypes.bfloat16).astype(np.float64).reshape(n // 32, 32, m)
    top = np.abs(v).max(1)
    byte = np.clip(np.where(top > 0, np.frexp(top)[1] - 1 + 127 - 7, 1), 1, 254)
    codes = (v * np.exp2(127.0 - byte)[:, None, :]).reshape(n, m).astype(np.float32).astype(ml_dtypes.float8_e4m3fn).view(np.uint8)
    words = codes.reshape(n // 512, 128, 4, m).transpose(0, 1, 3, 2)
    return np.ascontiguousarray(words), np.ascontiguousarray(byte.astype(np.uint8).reshape(n // 512, 16, m))


K, T, S, N, H = 512, 2048, 512, 512, 512


def setup_inputs():
    n = np.random.standard_normal
    s = mx_kscale(K)[:, None]
    u = mx_kscale(H)
    packed_xT = pack_weight(n((K, T)) * s)
    packed_w1 = pack_fp4(n((K, H)) / np.sqrt(K) / s)
    packed_w2 = pack_fp4(n((K, H)) / np.sqrt(K) / s)
    packed_w3 = pack_fp4(n((H, N)) / np.sqrt(2 * H) / u[:, None])
    packed_w4 = pack_fp4(n((H, N)) / np.sqrt(2 * H) / u[:, None])
    return {
        "x_words": packed_xT[0],
        "x_scales": packed_xT[1],
        "w1_words": packed_w1[0],
        "w1_scales": packed_w1[1],
        "w2_words": packed_w2[0],
        "w2_scales": packed_w2[1],
        "gn": (np.random.uniform(0.5, 1.5, (H, 1)) * u[:, None]).astype(np.float32),
        "gm": (np.random.uniform(0.5, 1.5, (H, 1)) * u[:, None]).astype(np.float32),
        "w3_words": packed_w3[0],
        "w3_scales": packed_w3[1],
        "w4_words": packed_w4[0],
        "w4_scales": packed_w4[1],
        "offs": striped(np.random.permutation(T)[:S]),
        "hz": striped8(np.random.randint(0, T, (8, S))),
        "n1": striped8(np.stack([np.random.permutation(S) for _ in range(8)])),
        "n2": striped8(np.stack([np.random.permutation(S) for _ in range(8)])),
        "n3": striped(np.random.permutation(S)),
        "n4": striped(np.random.permutation(S)),
        "n5": striped8(np.stack([np.random.permutation(S) for _ in range(8)])),
    }


def reference(x_words, x_scales, w1_words, w1_scales, w2_words, w2_scales, gn, gm, w3_words, w3_scales, w4_words, w4_scales, offs, hz, n1, n2, n3, n4, n5):
    xq = unpack_weight(x_words, x_scales)[:, unstriped(offs)]
    y = unpack_fp4(w1_words, w1_scales).T @ xq
    z = f64(gn) * (y * (sigmoid(y[np.arange(H)[:, None], runs(n1, H)] - (y[np.arange(H)[:, None], runs(n2, H)]))))
    x_hz = unpack_weight(x_words, x_scales)[np.arange(K)[:, None], runs(hz, K)]
    d = unpack_fp4(w2_words, w2_scales).T @ x_hz
    z2 = f64(gm) * (np.minimum(np.maximum(d, d[:, unstriped(n3)]), d[:, unstriped(n4)]))
    h = unpack_fp4(w3_words, w3_scales).T @ mxq(z, 0, "e4m3") + unpack_fp4(w4_words, w4_scales).T @ mxq(z2, 0, "e4m3")
    out_0 = h - (h[np.arange(N)[:, None], runs(n5, N)])
    return (out_0,) + planes(out_0)

@@ -1,0 +1,250 @@
+from contextlib import ExitStack
+
+import concourse.mybir as mybir
+
+K, T, S, H, N = 512, 2048, 512, 512, 512
+FLOPS = 4 * 2 * 512 * 512 * 512
+
+F32 = mybir.dt.float32
+BF16 = mybir.dt.bfloat16
+I32 = mybir.dt.int32
+U32 = mybir.dt.uint32
+U16 = mybir.dt.uint16
+U8 = mybir.dt.uint8
+FP8X4 = mybir.dt.float8_e4m3fn_x4
+FP4X4 = mybir.dt.float4_e2m1fn_x4
+ALU = mybir.AluOpType
+ACT = mybir.ActivationFunctionType
+
+P = 128
+PACK = 4
+HALVES = (slice(0, 256), slice(256, 512))
+TAIL_CHUNKS = (slice(0, 256), slice(256, 384), slice(384, 512))
+
+
+def tile_picked_hjoincmpminmxdif_none_po_kernel(
+    tc, x_words, x_scales, w1_words, w1_scales, w2_words, w2_scales, gn, gm,
+    w3_words, w3_scales, w4_words, w4_scales, offs, hz, n1, n2, n3, n4, n5,
+    out_0, out_1, out_2,
+):
+    nc = tc.nc
+    with ExitStack() as ctx:
+        keep = ctx.enter_context(tc.tile_pool(name="keep", bufs=1))
+        psum = ctx.enter_context(tc.psum_pool(name="psum", bufs=1))
+
+        def sb(name, shape, dtype):
+            return keep.tile(shape, dtype, name=name, align_bytes=64)
+
+        def load_list(name, dram):
+            tile = keep.tile([P, S // 16], U16, name=name)
+            nc.sync.dma_start(tile[:], dram)
+            return tile
+
+        def entries(tile, cols):
+            return tile[:, cols.start // 16 : cols.stop // 16]
+
+        def load_scale_rows(tile, dram, queue):
+            for r in range(4):
+                queue.dma_start(tile[r:P:32, :].bitcast(I32), dram[0, r:16:4, :].bitcast(I32))
+
+        def load_words(name, words):
+            raw = sb(name + "_raw_words", [P, 2 * H], U8)
+            nc.scalar.dma_start(raw[:].bitcast(I32), words[0].bitcast(I32))
+            dealt = sb(name + "_words", [P, 2 * H], U8)
+            nc.scalar.copy(
+                dealt[:].bitcast(U16).rearrange("p (t m) -> p t m", t=PACK),
+                raw[:].bitcast(U16).rearrange("p (m t) -> p t m", t=PACK),
+            )
+            return dealt
+
+        def load_scales(name, scales):
+            raw = sb(name + "_raw_scales", [P, H], U8)
+            nc.gpsimd.memset(raw[:].bitcast(I32), 0)
+            load_scale_rows(raw, scales, nc.sync)
+            dealt = sb(name + "_scales", [P, H], U8)
+            nc.gpsimd.tensor_copy(
+                dealt[:].rearrange("p (t m) -> p t m", t=PACK),
+                raw[:].rearrange("p (m t) -> p t m", t=PACK),
+            )
+            return dealt
+
+        def product(bank, weight, t, codes, scales, cols, start, stop):
+            words, wscales = weight
+            nc.tensor.matmul_mx(
+                out=bank,
+                lhsT=words[:, 2 * P * t : 2 * P * (t + 1)].bitcast(FP4X4),
+                lhsT_scale=wscales[:, P * t : P * (t + 1)],
+                rhs=codes[:, cols].bitcast(FP8X4),
+                rhs_scale=scales[:, cols],
+                start=start,
+                stop=stop,
+            )
+
+        def rows_view(tile, cols):
+            return tile[:, :, cols].rearrange("p t (c i) -> p c t i", i=4)
+
+        def woven_view(tile, cols):
+            return tile[:, PACK * cols.start : PACK * cols.stop].rearrange("p (c i t) -> p c t i", i=4, t=PACK)
+
+        def quantize(codes, scales, woven, cols):
+            nc.vector.quantize_mx(
+                out=codes[:, cols].bitcast(FP8X4),
+                scales=scales[:, cols],
+                in_=woven[:, PACK * cols.start : PACK * cols.stop],
+            )
+
+        whole = slice(0, S)
+
+        xw = sb("xw", [P, T], I32)
+        xs_one = sb("xs_one", [P, T], U8)
+        xs_runs = sb("xs_runs", [P, T], U8)
+        nc.vector.memset(xs_one[:].bitcast(I32), 0)
+        nc.vector.memset(xs_runs[:].bitcast(I32), 0)
+        nc.scalar.dma_start(xw[:], x_words[0].rearrange("p c r -> p (c r)").bitcast(I32))
+        offs_l = load_list("offs_l", offs)
+        load_scale_rows(xs_one, x_scales, nc.sync)
+        w1_dealt = load_words("w1", w1_words)
+        w1 = (w1_dealt, load_scales("w1", w1_scales))
+        warm = sb("warm", [P, 1], F32)
+        nc.gpsimd.memset(warm[:], 0.0)
+        warm_out = sb("warm_out", [P, 1], F32)
+        nc.scalar.activation(warm_out[:], warm[:], ACT.Sigmoid)
+
+        qs = sb("qs", [P, S], U8)
+        nc.vector.tensor_copy(qs[:], xs_one[:].indirect(offs_l[:]))
+        qw = sb("qw", [P, S], U32)
+        nc.vector.tensor_copy(qw[:], xw[:].bitcast(U32).indirect(offs_l[:]))
+        y_ps = [psum.tile([P, S], F32, name="y_ps%d" % t, tag="a%d" % t) for t in range(PACK)]
+        for t in range(PACK):
+            product(y_ps[t][:], w1, t, qw, qs, whole, True, True)
+
+        hz_l = load_list("hz_l", hz)
+        for r in range(4):
+            first = r if r < 2 else 14 + r
+            nc.sync.dma_start(xs_runs[first:P:32, :].bitcast(I32), x_scales[0, r:16:4, :].bitcast(I32))
+        w2_dealt = load_words("w2", w2_words)
+        w3_dealt = load_words("w3", w3_words)
+        w4_dealt = load_words("w4", w4_words)
+        n1_l = load_list("n1_l", n1)
+        n2_l = load_list("n2_l", n2)
+        w2 = (w2_dealt, load_scales("w2", w2_scales))
+
+        hs_raw = sb("hs_raw", [P, S], U8)
+        hs = sb("hs", [P, S], U8)
+        nc.vector.tensor_copy(hs_raw[:], xs_runs[:].indirect(hz_l[:]))
+        nc.vector.tensor_copy(hs[:].bitcast(I32), hs_raw[:].bitcast(I32))
+        for r in (2, 3):
+            nc.sync.dma_start(hs[r:P:32, :].bitcast(I32), hs_raw[14 + r : P : 32, :].bitcast(I32))
+        hw = sb("hw", [P, S], U32)
+        nc.vector.tensor_copy(hw[:], xw[:].bitcast(U32).indirect(hz_l[:]))
+        d_ps = [psum.tile([P, S], F32, name="d_ps%d" % t, tag="b%d" % t) for t in range(PACK)]
+        for t in range(PACK):
+            product(d_ps[t][:], w2, t, hw, hs, whole, True, True)
+
+        gn_sb = sb("gn_sb", [P, PACK], F32)
+        nc.sync.dma_start(gn_sb[:], gn.rearrange("(p t) o -> p (t o)", t=PACK))
+        gm_sb = sb("gm_sb", [P, PACK], F32)
+        nc.sync.dma_start(gm_sb[:], gm.rearrange("(p t) o -> p (t o)", t=PACK))
+        n3_l = load_list("n3_l", n3)
+        n4_l = load_list("n4_l", n4)
+        w3 = (w3_dealt, load_scales("w3", w3_scales))
+        w4 = (w4_dealt, load_scales("w4", w4_scales))
+        n5_l = load_list("n5_l", n5)
+
+        gm_twice = sb("gm_twice", [P, PACK], F32)
+        gm_sign = sb("gm_sign", [P, PACK], BF16)
+        gm_size = sb("gm_size", [P, PACK], F32)
+        nc.gpsimd.tensor_scalar(gm_twice[:], gm_sb[:], 0.0, 2.0, ALU.is_ge, ALU.mult)
+        nc.gpsimd.tensor_scalar(gm_sign[:], gm_twice[:], 1.0, -1.0, ALU.mult, ALU.add)
+        nc.gpsimd.tensor_tensor(gm_size[:], gm_sb[:], gm_sign[:], ALU.mult)
+
+        y = [sb("y_win%d" % t, [P, S], F32) for t in range(PACK)]
+        d = [sb("d_win%d" % t, [P, S], F32) for t in range(PACK)]
+        y1 = [sb("y1_%d" % t, [P, S], F32) for t in range(PACK)]
+        diff = [sb("diff%d" % t, [P, S], F32) for t in range(PACK)]
+        gate = [sb("gate%d" % t, [P, S], F32) for t in range(PACK)]
+        z_rows = sb("z_rows", [P, PACK, S], BF16)
+
+        def gate_step(t):
+            nc.scalar.activation(gate[t][:], diff[t][:], ACT.Sigmoid, scale=-1.0)
+            nc.vector.scalar_tensor_tensor(
+                z_rows[:, t, :], y_ps[t][:], gn_sb[:, t : t + 1], gate[t][:], ALU.mult, ALU.mult
+            )
+            nc.vector.tensor_scalar(d[t][:], d_ps[t][:], gm_size[:, t : t + 1], None, ALU.mult)
+
+        for t in range(PACK):
+            nc.scalar.copy(y[t][:], y_ps[t][:])
+            for cols in HALVES:
+                nc.scalar.activation(y1[t][:, cols], y[t][:].indirect(entries(n1_l, cols)), ACT.Copy)
+            for cols in HALVES:
+                nc.vector.tensor_tensor(
+                    diff[t][:, cols], y[t][:].indirect(entries(n2_l, cols)), y1[t][:, cols], ALU.subtract
+                )
+            if t > 0:
+                gate_step(t - 1)
+        gate_step(PACK - 1)
+
+        z_woven = sb("z_woven", [P, PACK * S], BF16)
+        z_codes = sb("z_codes", [P, S], U32)
+        z_scales = sb("z_scales", [P, S], U8)
+        nc.vector.tensor_copy(woven_view(z_woven, whole), rows_view(z_rows, whole))
+
+        d3 = sb("d3", [P, PACK, S], F32)
+        d4 = sb("d4", [P, PACK, S], F32)
+        upper = sb("upper", [P, PACK, S], F32)
+        z2_size = sb("z2_size", [P, PACK * S], BF16)
+        z2_woven = sb("z2_woven", [P, PACK * S], BF16)
+        z2_codes = sb("z2_codes", [P, S], U32)
+        z2_scales = sb("z2_scales", [P, S], U8)
+        h = [sb("h_win%d" % t, [P, S], F32) for t in range(PACK)]
+        h_ps = {}
+        for c, cols in enumerate(HALVES):
+            for t in range(PACK):
+                nc.scalar.activation(d3[:, t, cols], d[t][:].indirect(entries(n3_l, cols)), ACT.Copy)
+                nc.scalar.activation(d4[:, t, cols], d[t][:].indirect(entries(n4_l, cols)), ACT.Copy)
+                nc.vector.tensor_tensor(upper[:, t, cols], d[t][:, cols], d3[:, t, cols], ALU.max)
+                if c == 0 and t == 0:
+                    quantize(z_codes, z_scales, z_woven, whole)
+            width = cols.stop - cols.start
+            nc.vector.tensor_tensor(woven_view(z2_size, cols), rows_view(upper, cols), rows_view(d4, cols), ALU.min)
+            span = slice(PACK * cols.start, PACK * cols.stop)
+            nc.vector.tensor_tensor(
+                z2_woven[:, span].rearrange("p (j t) -> p j t", t=PACK),
+                z2_size[:, span].rearrange("p (j t) -> p j t", t=PACK),
+                gm_sign[:].unsqueeze(1).broadcast_to([P, width, PACK]),
+                ALU.mult,
+            )
+            quantize(z2_codes, z2_scales, z2_woven, cols)
+            for t in range(PACK):
+                bank = psum.tile([P, width], F32, name="h_ps%d_%d" % (c, t), tag="%s%d" % ("ab"[c], t))
+                h_ps[c, t] = bank
+                product(bank[:], w3, t, z_codes, z_scales, cols, True, False)
+                product(bank[:], w4, t, z2_codes, z2_scales, cols, False, True)
+            for t in range(PACK):
+                if c == 1 and t % 2 == 1:
+                    nc.vector.tensor_copy(h[t][:, cols], h_ps[c, t][:])
+                else:
+                    nc.scalar.copy(h[t][:, cols], h_ps[c, t][:])
+
+        h5 = sb("h5", [P, PACK, S], F32)
+        res = sb("res", [P, PACK, S], F32)
+        res_woven = sb("res_woven", [P, PACK * S], BF16)
+        res_codes = sb("res_codes", [P, S], I32)
+        res_scales = sb("res_scales", [P, S], U8)
+        out_rows = out_0.rearrange("(p t) j -> p t j", t=PACK)
+        out_words = out_1[0].rearrange("p c r -> p (c r)").bitcast(I32)
+        for c, cols in enumerate(TAIL_CHUNKS):
+            for t in range(PACK):
+                if c == 0 and t % 2 == 1:
+                    nc.vector.tensor_copy(h5[:, t, cols], h[t][:].indirect(entries(n5_l, cols)))
+                else:
+                    nc.scalar.activation(h5[:, t, cols], h[t][:].indirect(entries(n5_l, cols)), ACT.Copy)
+            for t in range(PACK):
+                nc.vector.tensor_tensor(res[:, t, cols], h[t][:, cols], h5[:, t, cols], ALU.subtract)
+            nc.sync.dma_start(out_rows[:, :, cols], res[:, :, cols])
+            nc.vector.tensor_copy(woven_view(res_woven, cols), rows_view(res, cols))
+            quantize(res_codes, res_scales, res_woven, cols)
+            nc.sync.dma_start(out_words[:, cols], res_codes[:, cols])
+        for r in range(4):
+            queue = nc.scalar if r % 2 else nc.sync
+            queue.dma_start(out_2[0, r:16:4, :].bitcast(I32), res_scales[r:P:32, :].bitcast(I32))

@@ -19,7 +19,12 @@ ACT = mybir.ActivationFunctionType
 P = 128
 PACK = 4
 HALVES = (slice(0, 256), slice(256, 512))
-TAIL_CHUNKS = (slice(0, 256), slice(256, 384), slice(384, 512))
+Y_ROWS_ON_VECTOR = (0,)
+Y1_ON_VECTOR = (0,)
+H5_ON_VECTOR = (2,3)
+LAG = 3
+D4_ON_VECTOR = 2
+CHUNKS = (slice(0, 256), slice(256, 384), slice(384, 512))
 
 
 def tile_picked_hjoincmpminmxdif_none_po_kernel(
@@ -43,29 +48,40 @@ def tile_picked_hjoincmpminmxdif_none_po_kernel(
         def entries(tile, cols):
             return tile[:, cols.start // 16 : cols.stop // 16]
 
-        def load_scale_rows(tile, dram, queue):
-            for r in range(4):
-                queue.dma_start(tile[r:P:32, :].bitcast(I32), dram[0, r:16:4, :].bitcast(I32))
+        def load_scale_rows(rows, dram, queue):
+            queue.dma_start(rows[0:P:8, :].bitcast(I32), dram[0].bitcast(I32))
 
-        def load_words(name, words):
-            raw = sb(name + "_raw_words", [P, 2 * H], U8)
-            nc.scalar.dma_start(raw[:].bitcast(I32), words[0].bitcast(I32))
-            dealt = sb(name + "_words", [P, 2 * H], U8)
-            nc.scalar.copy(
-                dealt[:].bitcast(U16).rearrange("p (t m) -> p t m", t=PACK),
-                raw[:].bitcast(U16).rearrange("p (m t) -> p t m", t=PACK),
-            )
-            return dealt
+        def place_scale_rows(plane, rows, queue):
+            for r in range(1, 4):
+                queue.dma_start(plane[r:P:32, :].bitcast(I32), rows[8 * r : P : 32, :].bitcast(I32))
 
-        def load_scales(name, scales):
-            raw = sb(name + "_raw_scales", [P, H], U8)
-            nc.gpsimd.memset(raw[:].bitcast(I32), 0)
-            load_scale_rows(raw, scales, nc.sync)
-            dealt = sb(name + "_scales", [P, H], U8)
+        def deal_scales(dealt, raw):
             nc.gpsimd.tensor_copy(
-                dealt[:].rearrange("p (t m) -> p t m", t=PACK),
-                raw[:].rearrange("p (m t) -> p t m", t=PACK),
+                dealt.rearrange("p (t m) -> p t m", t=PACK), raw.rearrange("p (m t) -> p t m", t=PACK)
             )
+
+        def gather_scales(name, window, offsets, queue):
+            picked = sb(name + "_picked", [P, S], U8)
+            plane = sb(name, [P, S], U8)
+            nc.vector.tensor_copy(picked[:], window[:].indirect(offsets[:]))
+            nc.vector.tensor_copy(plane[:].bitcast(I32), picked[:].bitcast(I32))
+            place_scale_rows(plane, picked, queue)
+            return plane
+
+        def load_words(name, words, queue, on_scalar):
+            raw = sb(name + "_raw_words", [P, 2 * H], U8)
+            queue.dma_start(raw[:].bitcast(I32), words[0].bitcast(I32))
+            dealt = sb(name + "_words", [P, 2 * H], U8)
+            if on_scalar:
+                nc.scalar.copy(
+                    dealt[:].bitcast(U16).rearrange("p (t m) -> p t m", t=PACK),
+                    raw[:].bitcast(U16).rearrange("p (m t) -> p t m", t=PACK),
+                )
+            else:
+                nc.gpsimd.tensor_copy(
+                    dealt[:].rearrange("p (t m b) -> p t m b", t=PACK, b=2),
+                    raw[:].rearrange("p (m t b) -> p t m b", t=PACK, b=2),
+                )
             return dealt
 
         def product(bank, weight, t, codes, scales, cols, start, stop):
@@ -98,58 +114,74 @@ def tile_picked_hjoincmpminmxdif_none_po_kernel(
         xw = sb("xw", [P, T], I32)
         xs_one = sb("xs_one", [P, T], U8)
         xs_runs = sb("xs_runs", [P, T], U8)
+        first_raw = sb("first_raw", [P, H], U8)
+        second_raw = sb("second_raw", [P, H], U8)
+        later_raw = sb("later_raw", [P, 2 * H], U8)
         nc.vector.memset(xs_one[:].bitcast(I32), 0)
         nc.vector.memset(xs_runs[:].bitcast(I32), 0)
-        nc.scalar.dma_start(xw[:], x_words[0].rearrange("p c r -> p (c r)").bitcast(I32))
+        nc.gpsimd.memset(later_raw[:].bitcast(I32), 0)
+        nc.gpsimd.memset(second_raw[:].bitcast(I32), 0)
+        nc.gpsimd.memset(first_raw[:].bitcast(I32), 0)
         offs_l = load_list("offs_l", offs)
-        load_scale_rows(xs_one, x_scales, nc.sync)
-        w1_dealt = load_words("w1", w1_words)
-        w1 = (w1_dealt, load_scales("w1", w1_scales))
+        for r in range(4):
+            queue = nc.sync if r < 2 else nc.scalar
+            queue.dma_start(xs_one[r:P:32, :].bitcast(I32), x_scales[0, r:16:4, :].bitcast(I32))
+        hz_l = load_list("hz_l", hz)
+        load_scale_rows(xs_runs, x_scales, nc.scalar)
+        nc.sync.dma_start(xw[:], x_words[0].rearrange("p c r -> p (c r)").bitcast(I32))
+        for r in range(4):
+            nc.scalar.dma_start(first_raw[r:P:32, :].bitcast(I32), w1_scales[0, r:16:4, :].bitcast(I32))
+        w1_dealt = load_words("w1", w1_words, nc.sync, True)
         warm = sb("warm", [P, 1], F32)
         nc.gpsimd.memset(warm[:], 0.0)
         warm_out = sb("warm_out", [P, 1], F32)
         nc.scalar.activation(warm_out[:], warm[:], ACT.Sigmoid)
 
+        first_scales = sb("first_scales", [P, H], U8)
+        deal_scales(first_scales[:], first_raw[:])
+        w1 = (w1_dealt, first_scales)
+
         qs = sb("qs", [P, S], U8)
         nc.vector.tensor_copy(qs[:], xs_one[:].indirect(offs_l[:]))
+        hs = gather_scales("hs", xs_runs, hz_l, nc.scalar)
         qw = sb("qw", [P, S], U32)
         nc.vector.tensor_copy(qw[:], xw[:].bitcast(U32).indirect(offs_l[:]))
         y_ps = [psum.tile([P, S], F32, name="y_ps%d" % t, tag="a%d" % t) for t in range(PACK)]
         for t in range(PACK):
             product(y_ps[t][:], w1, t, qw, qs, whole, True, True)
 
-        hz_l = load_list("hz_l", hz)
-        for r in range(4):
-            first = r if r < 2 else 14 + r
-            nc.sync.dma_start(xs_runs[first:P:32, :].bitcast(I32), x_scales[0, r:16:4, :].bitcast(I32))
-        w2_dealt = load_words("w2", w2_words)
-        w3_dealt = load_words("w3", w3_words)
-        w4_dealt = load_words("w4", w4_words)
         n1_l = load_list("n1_l", n1)
         n2_l = load_list("n2_l", n2)
-        w2 = (w2_dealt, load_scales("w2", w2_scales))
+        w2_dealt = load_words("w2", w2_words, nc.sync, True)
+        for r in range(4):
+            nc.sync.dma_start(second_raw[r:P:32, :].bitcast(I32), w2_scales[0, r:16:4, :].bitcast(I32))
+        second_scales = sb("second_scales", [P, H], U8)
+        deal_scales(second_scales[:], second_raw[:])
+        w2 = (w2_dealt, second_scales)
 
-        hs_raw = sb("hs_raw", [P, S], U8)
-        hs = sb("hs", [P, S], U8)
-        nc.vector.tensor_copy(hs_raw[:], xs_runs[:].indirect(hz_l[:]))
-        nc.vector.tensor_copy(hs[:].bitcast(I32), hs_raw[:].bitcast(I32))
-        for r in (2, 3):
-            nc.sync.dma_start(hs[r:P:32, :].bitcast(I32), hs_raw[14 + r : P : 32, :].bitcast(I32))
         hw = sb("hw", [P, S], U32)
         nc.vector.tensor_copy(hw[:], xw[:].bitcast(U32).indirect(hz_l[:]))
         d_ps = [psum.tile([P, S], F32, name="d_ps%d" % t, tag="b%d" % t) for t in range(PACK)]
         for t in range(PACK):
             product(d_ps[t][:], w2, t, hw, hs, whole, True, True)
 
-        gn_sb = sb("gn_sb", [P, PACK], F32)
-        nc.sync.dma_start(gn_sb[:], gn.rearrange("(p t) o -> p (t o)", t=PACK))
         gm_sb = sb("gm_sb", [P, PACK], F32)
         nc.sync.dma_start(gm_sb[:], gm.rearrange("(p t) o -> p (t o)", t=PACK))
+        gn_sb = sb("gn_sb", [P, PACK], F32)
+        nc.sync.dma_start(gn_sb[:], gn.rearrange("(p t) o -> p (t o)", t=PACK))
         n3_l = load_list("n3_l", n3)
         n4_l = load_list("n4_l", n4)
-        w3 = (w3_dealt, load_scales("w3", w3_scales))
-        w4 = (w4_dealt, load_scales("w4", w4_scales))
+        w3_dealt = load_words("w3", w3_words, nc.sync, False)
+        w4_dealt = load_words("w4", w4_words, nc.sync, False)
         n5_l = load_list("n5_l", n5)
+        later_scales = sb("later_scales", [P, 2 * H], U8)
+        parts = [slice(H * i, H * (i + 1)) for i in range(2)]
+        for part, dram in zip(parts, (w3_scales, w4_scales)):
+            load_scale_rows(later_raw[:, part], dram, nc.sync)
+            deal_scales(later_scales[:, part], later_raw[:, part])
+        place_scale_rows(later_scales, later_scales, nc.sync)
+        w3 = (w3_dealt, later_scales[:, parts[0]])
+        w4 = (w4_dealt, later_scales[:, parts[1]])
 
         gm_twice = sb("gm_twice", [P, PACK], F32)
         gm_sign = sb("gm_sign", [P, PACK], BF16)
@@ -159,53 +191,93 @@ def tile_picked_hjoincmpminmxdif_none_po_kernel(
         nc.gpsimd.tensor_tensor(gm_size[:], gm_sb[:], gm_sign[:], ALU.mult)
 
         y = [sb("y_win%d" % t, [P, S], F32) for t in range(PACK)]
-        d = [sb("d_win%d" % t, [P, S], F32) for t in range(PACK)]
+        d = sb("d_win", [P, PACK, S], F32)
         y1 = [sb("y1_%d" % t, [P, S], F32) for t in range(PACK)]
         diff = [sb("diff%d" % t, [P, S], F32) for t in range(PACK)]
         gate = [sb("gate%d" % t, [P, S], F32) for t in range(PACK)]
         z_rows = sb("z_rows", [P, PACK, S], BF16)
+        d3 = sb("d3", [P, PACK, S], F32)
+        d4 = sb("d4", [P, PACK, S], F32)
 
-        def gate_step(t):
-            nc.scalar.activation(gate[t][:], diff[t][:], ACT.Sigmoid, scale=-1.0)
-            nc.vector.scalar_tensor_tensor(
-                z_rows[:, t, :], y_ps[t][:], gn_sb[:, t : t + 1], gate[t][:], ALU.mult, ALU.mult
-            )
-            nc.vector.tensor_scalar(d[t][:], d_ps[t][:], gm_size[:, t : t + 1], None, ALU.mult)
+        def fetch(on_vector, out, window, offsets):
+            if on_vector:
+                nc.vector.tensor_copy(out, window.indirect(offsets))
+            else:
+                nc.scalar.activation(out, window.indirect(offsets), ACT.Copy)
 
-        for t in range(PACK):
-            nc.scalar.copy(y[t][:], y_ps[t][:])
+        def difference(t):
+            if t in Y_ROWS_ON_VECTOR:
+                nc.vector.tensor_copy(y[t][:], y_ps[t][:])
+            else:
+                nc.scalar.copy(y[t][:], y_ps[t][:])
             for cols in HALVES:
-                nc.scalar.activation(y1[t][:, cols], y[t][:].indirect(entries(n1_l, cols)), ACT.Copy)
+                fetch(t in Y1_ON_VECTOR, y1[t][:, cols], y[t][:], entries(n1_l, cols))
             for cols in HALVES:
                 nc.vector.tensor_tensor(
                     diff[t][:, cols], y[t][:].indirect(entries(n2_l, cols)), y1[t][:, cols], ALU.subtract
                 )
-            if t > 0:
-                gate_step(t - 1)
-        gate_step(PACK - 1)
+
+        def gated(t):
+            nc.scalar.activation(gate[t][:], diff[t][:], ACT.Sigmoid, scale=-1.0)
+            nc.vector.scalar_tensor_tensor(
+                z_rows[:, t, :], y_ps[t][:], gn_sb[:, t : t + 1], gate[t][:], ALU.mult, ALU.mult
+            )
+
+        def d_rows(t):
+            nc.scalar.activation(d[:, t, :], d_ps[t][:], ACT.Copy, scale=gm_size[:, t : t + 1])
+            fetch(False, d3[:, t, CHUNKS[0]], d[:, t, :], entries(n3_l, CHUNKS[0]))
+
+        for step in range(PACK + LAG):
+            if step < PACK:
+                difference(step)
+            else:
+                d_rows(step - PACK)
+            if step >= LAG:
+                gated(step - LAG)
+        for t in range(LAG, PACK):
+            d_rows(t)
 
         z_woven = sb("z_woven", [P, PACK * S], BF16)
         z_codes = sb("z_codes", [P, S], U32)
         z_scales = sb("z_scales", [P, S], U8)
         nc.vector.tensor_copy(woven_view(z_woven, whole), rows_view(z_rows, whole))
+        for t in range(D4_ON_VECTOR):
+            fetch(True, d4[:, t, CHUNKS[0]], d[:, t, :], entries(n4_l, CHUNKS[0]))
+        quantize(z_codes, z_scales, z_woven, whole)
 
-        d3 = sb("d3", [P, PACK, S], F32)
-        d4 = sb("d4", [P, PACK, S], F32)
+        h_ps = {}
+        free_banks = ["b0", "b1", "b2", "b3", "a0", "a1"]
+        for c, cols in enumerate(CHUNKS):
+            width = cols.stop - cols.start
+            for u in range(2):
+                bank = psum.tile([P, 2, width], F32, name="h_ps%d_%d" % (c, u), tag=free_banks[2 * c + u])
+                h_ps[c, u] = bank
+                for e in range(2):
+                    product(bank[:, e, :], w3, 2 * u + e, z_codes, z_scales, cols, e == 0, False)
+
         upper = sb("upper", [P, PACK, S], F32)
         z2_size = sb("z2_size", [P, PACK * S], BF16)
         z2_woven = sb("z2_woven", [P, PACK * S], BF16)
         z2_codes = sb("z2_codes", [P, S], U32)
         z2_scales = sb("z2_scales", [P, S], U8)
         h = [sb("h_win%d" % t, [P, S], F32) for t in range(PACK)]
-        h_ps = {}
-        for c, cols in enumerate(HALVES):
+
+        def h_rows(c):
+            cols = CHUNKS[c]
             for t in range(PACK):
-                nc.scalar.activation(d3[:, t, cols], d[t][:].indirect(entries(n3_l, cols)), ACT.Copy)
-                nc.scalar.activation(d4[:, t, cols], d[t][:].indirect(entries(n4_l, cols)), ACT.Copy)
-                nc.vector.tensor_tensor(upper[:, t, cols], d[t][:, cols], d3[:, t, cols], ALU.max)
-                if c == 0 and t == 0:
-                    quantize(z_codes, z_scales, z_woven, whole)
+                if c == len(CHUNKS) - 1 and t >= 2:
+                    nc.vector.tensor_copy(h[t][:, cols], h_ps[c, t // 2][:, t % 2, :])
+                else:
+                    nc.scalar.copy(h[t][:, cols], h_ps[c, t // 2][:, t % 2, :])
+
+        for c, cols in enumerate(CHUNKS):
             width = cols.stop - cols.start
+            if c > 0:
+                for t in range(PACK):
+                    fetch(False, d3[:, t, cols], d[:, t, :], entries(n3_l, cols))
+            nc.vector.tensor_tensor(upper[:, :, cols], d[:, :, cols], d3[:, :, cols], ALU.max)
+            for t in range(D4_ON_VECTOR if c == 0 else 0, PACK):
+                fetch(False, d4[:, t, cols], d[:, t, :], entries(n4_l, cols))
             nc.vector.tensor_tensor(woven_view(z2_size, cols), rows_view(upper, cols), rows_view(d4, cols), ALU.min)
             span = slice(PACK * cols.start, PACK * cols.stop)
             nc.vector.tensor_tensor(
@@ -216,15 +288,9 @@ def tile_picked_hjoincmpminmxdif_none_po_kernel(
             )
             quantize(z2_codes, z2_scales, z2_woven, cols)
             for t in range(PACK):
-                bank = psum.tile([P, width], F32, name="h_ps%d_%d" % (c, t), tag="%s%d" % ("ab"[c], t))
-                h_ps[c, t] = bank
-                product(bank[:], w3, t, z_codes, z_scales, cols, True, False)
-                product(bank[:], w4, t, z2_codes, z2_scales, cols, False, True)
-            for t in range(PACK):
-                if c == 1 and t % 2 == 1:
-                    nc.vector.tensor_copy(h[t][:, cols], h_ps[c, t][:])
-                else:
-                    nc.scalar.copy(h[t][:, cols], h_ps[c, t][:])
+                product(h_ps[c, t // 2][:, t % 2, :], w4, t, z2_codes, z2_scales, cols, False, t % 2 == 1)
+        for c in range(len(CHUNKS)):
+            h_rows(c)
 
         h5 = sb("h5", [P, PACK, S], F32)
         res = sb("res", [P, PACK, S], F32)
@@ -233,14 +299,12 @@ def tile_picked_hjoincmpminmxdif_none_po_kernel(
         res_scales = sb("res_scales", [P, S], U8)
         out_rows = out_0.rearrange("(p t) j -> p t j", t=PACK)
         out_words = out_1[0].rearrange("p c r -> p (c r)").bitcast(I32)
-        for c, cols in enumerate(TAIL_CHUNKS):
+        for c, cols in enumerate(CHUNKS):
             for t in range(PACK):
-                if c == 0 and t % 2 == 1:
-                    nc.vector.tensor_copy(h5[:, t, cols], h[t][:].indirect(entries(n5_l, cols)))
-                else:
-                    nc.scalar.activation(h5[:, t, cols], h[t][:].indirect(entries(n5_l, cols)), ACT.Copy)
-            for t in range(PACK):
-                nc.vector.tensor_tensor(res[:, t, cols], h[t][:, cols], h5[:, t, cols], ALU.subtract)
+                fetch(c == 0 and t in H5_ON_VECTOR, h5[:, t, cols], h[t][:], entries(n5_l, cols))
+            for u in range(2):
+                pair = slice(2 * u, 2 * u + 2)
+                nc.vector.tensor_tensor(res[:, pair, cols], h_ps[c, u][:], h5[:, pair, cols], ALU.subtract)
             nc.sync.dma_start(out_rows[:, :, cols], res[:, :, cols])
             nc.vector.tensor_copy(woven_view(res_woven, cols), rows_view(res, cols))
             quantize(res_codes, res_scales, res_woven, cols)

@@ -19,11 +19,11 @@ ACT = mybir.ActivationFunctionType
 P = 128
 PACK = 4
 HALVES = (slice(0, 256), slice(256, 512))
-Y_ROWS_ON_VECTOR = (0,)
-Y1_ON_VECTOR = (0,)
+Y_ROWS_ON_VECTOR = ()
+Y1_ON_VECTOR = ()
 H5_ON_VECTOR = (2,3)
 LAG = 3
-D4_ON_VECTOR = 2
+D4_ON_VECTOR = 3
 CHUNKS = (slice(0, 256), slice(256, 384), slice(384, 512))
 
 
@@ -51,8 +51,8 @@ def tile_picked_hjoincmpminmxdif_none_po_kernel(
         def load_scale_rows(rows, dram, queue):
             queue.dma_start(rows[0:P:8, :].bitcast(I32), dram[0].bitcast(I32))
 
-        def place_scale_rows(plane, rows, queue):
-            for r in range(1, 4):
+        def place_scale_rows(plane, rows, queue, first):
+            for r in range(first, 4):
                 queue.dma_start(plane[r:P:32, :].bitcast(I32), rows[8 * r : P : 32, :].bitcast(I32))
 
         def deal_scales(dealt, raw):
@@ -63,9 +63,9 @@ def tile_picked_hjoincmpminmxdif_none_po_kernel(
         def gather_scales(name, window, offsets, queue):
             picked = sb(name + "_picked", [P, S], U8)
             plane = sb(name, [P, S], U8)
+            nc.gpsimd.memset(plane[:].bitcast(I32), 0)
             nc.vector.tensor_copy(picked[:], window[:].indirect(offsets[:]))
-            nc.vector.tensor_copy(plane[:].bitcast(I32), picked[:].bitcast(I32))
-            place_scale_rows(plane, picked, queue)
+            place_scale_rows(plane, picked, queue, 0)
             return plane
 
         def load_words(name, words, queue, on_scalar):
@@ -118,57 +118,57 @@ def tile_picked_hjoincmpminmxdif_none_po_kernel(
         second_raw = sb("second_raw", [P, H], U8)
         later_raw = sb("later_raw", [P, 2 * H], U8)
         nc.vector.memset(xs_one[:].bitcast(I32), 0)
-        nc.vector.memset(xs_runs[:].bitcast(I32), 0)
-        nc.gpsimd.memset(later_raw[:].bitcast(I32), 0)
-        nc.gpsimd.memset(second_raw[:].bitcast(I32), 0)
         nc.gpsimd.memset(first_raw[:].bitcast(I32), 0)
         offs_l = load_list("offs_l", offs)
-        for r in range(4):
-            queue = nc.sync if r < 2 else nc.scalar
-            queue.dma_start(xs_one[r:P:32, :].bitcast(I32), x_scales[0, r:16:4, :].bitcast(I32))
-        hz_l = load_list("hz_l", hz)
-        load_scale_rows(xs_runs, x_scales, nc.scalar)
         nc.sync.dma_start(xw[:], x_words[0].rearrange("p c r -> p (c r)").bitcast(I32))
         for r in range(4):
-            nc.scalar.dma_start(first_raw[r:P:32, :].bitcast(I32), w1_scales[0, r:16:4, :].bitcast(I32))
+            nc.scalar.dma_start(xs_one[r:P:32, :].bitcast(I32), x_scales[0, r:16:4, :].bitcast(I32))
         w1_dealt = load_words("w1", w1_words, nc.sync, True)
+        for r in range(4):
+            queue = nc.sync if r < 2 else nc.gpsimd
+            queue.dma_start(first_raw[r:P:32, :].bitcast(I32), w1_scales[0, r:16:4, :].bitcast(I32))
         warm = sb("warm", [P, 1], F32)
-        nc.gpsimd.memset(warm[:], 0.0)
+        nc.vector.memset(warm[:], 0.0)
         warm_out = sb("warm_out", [P, 1], F32)
         nc.scalar.activation(warm_out[:], warm[:], ACT.Sigmoid)
 
+        nc.vector.memset(xs_runs[:].bitcast(I32), 0)
+        nc.gpsimd.memset(second_raw[:].bitcast(I32), 0)
+        nc.gpsimd.memset(later_raw[:].bitcast(I32), 0)
         first_scales = sb("first_scales", [P, H], U8)
         deal_scales(first_scales[:], first_raw[:])
         w1 = (w1_dealt, first_scales)
 
         qs = sb("qs", [P, S], U8)
         nc.vector.tensor_copy(qs[:], xs_one[:].indirect(offs_l[:]))
-        hs = gather_scales("hs", xs_runs, hz_l, nc.scalar)
         qw = sb("qw", [P, S], U32)
         nc.vector.tensor_copy(qw[:], xw[:].bitcast(U32).indirect(offs_l[:]))
         y_ps = [psum.tile([P, S], F32, name="y_ps%d" % t, tag="a%d" % t) for t in range(PACK)]
         for t in range(PACK):
             product(y_ps[t][:], w1, t, qw, qs, whole, True, True)
 
+        hz_l = load_list("hz_l", hz)
+        load_scale_rows(xs_runs, x_scales, nc.sync)
         n1_l = load_list("n1_l", n1)
         n2_l = load_list("n2_l", n2)
-        w2_dealt = load_words("w2", w2_words, nc.sync, True)
+        gm_sb = sb("gm_sb", [P, PACK], F32)
+        nc.sync.dma_start(gm_sb[:], gm.rearrange("(p t) o -> p (t o)", t=PACK))
+        gn_sb = sb("gn_sb", [P, PACK], F32)
+        nc.sync.dma_start(gn_sb[:], gn.rearrange("(p t) o -> p (t o)", t=PACK))
+        w2_dealt = load_words("w2", w2_words, nc.sync, False)
         for r in range(4):
             nc.sync.dma_start(second_raw[r:P:32, :].bitcast(I32), w2_scales[0, r:16:4, :].bitcast(I32))
         second_scales = sb("second_scales", [P, H], U8)
         deal_scales(second_scales[:], second_raw[:])
         w2 = (w2_dealt, second_scales)
 
+        hs = gather_scales("hs", xs_runs, hz_l, nc.sync)
         hw = sb("hw", [P, S], U32)
         nc.vector.tensor_copy(hw[:], xw[:].bitcast(U32).indirect(hz_l[:]))
         d_ps = [psum.tile([P, S], F32, name="d_ps%d" % t, tag="b%d" % t) for t in range(PACK)]
         for t in range(PACK):
             product(d_ps[t][:], w2, t, hw, hs, whole, True, True)
 
-        gm_sb = sb("gm_sb", [P, PACK], F32)
-        nc.sync.dma_start(gm_sb[:], gm.rearrange("(p t) o -> p (t o)", t=PACK))
-        gn_sb = sb("gn_sb", [P, PACK], F32)
-        nc.sync.dma_start(gn_sb[:], gn.rearrange("(p t) o -> p (t o)", t=PACK))
         n3_l = load_list("n3_l", n3)
         n4_l = load_list("n4_l", n4)
         w3_dealt = load_words("w3", w3_words, nc.sync, False)
@@ -179,7 +179,7 @@ def tile_picked_hjoincmpminmxdif_none_po_kernel(
         for part, dram in zip(parts, (w3_scales, w4_scales)):
             load_scale_rows(later_raw[:, part], dram, nc.sync)
             deal_scales(later_scales[:, part], later_raw[:, part])
-        place_scale_rows(later_scales, later_scales, nc.sync)
+        place_scale_rows(later_scales, later_scales, nc.sync, 1)
         w3 = (w3_dealt, later_scales[:, parts[0]])
         w4 = (w4_dealt, later_scales[:, parts[1]])
 

from contextlib import ExitStack

import concourse.mybir as mybir

K, T, S, H, N = 512, 2048, 512, 512, 512
FLOPS = 4 * 2 * 512 * 512 * 512

F32 = mybir.dt.float32
BF16 = mybir.dt.bfloat16
I32 = mybir.dt.int32
U32 = mybir.dt.uint32
U16 = mybir.dt.uint16
U8 = mybir.dt.uint8
FP8X4 = mybir.dt.float8_e4m3fn_x4
FP4X4 = mybir.dt.float4_e2m1fn_x4
ALU = mybir.AluOpType
ACT = mybir.ActivationFunctionType

P = 128
PACK = 4
HALVES = (slice(0, 256), slice(256, 512))
Y_ROWS_ON_VECTOR = ()
Y1_ON_VECTOR = ()
H5_ON_VECTOR = (2,3)
LAG = 3
D4_ON_VECTOR = 3
CHUNKS = (slice(0, 256), slice(256, 384), slice(384, 512))


def tile_picked_hjoincmpminmxdif_none_po_kernel(
    tc, x_words, x_scales, w1_words, w1_scales, w2_words, w2_scales, gn, gm,
    w3_words, w3_scales, w4_words, w4_scales, offs, hz, n1, n2, n3, n4, n5,
    out_0, out_1, out_2,
):
    nc = tc.nc
    with ExitStack() as ctx:
        keep = ctx.enter_context(tc.tile_pool(name="keep", bufs=1))
        psum = ctx.enter_context(tc.psum_pool(name="psum", bufs=1))

        def sb(name, shape, dtype):
            return keep.tile(shape, dtype, name=name, align_bytes=64)

        def load_list(name, dram):
            tile = keep.tile([P, S // 16], U16, name=name)
            nc.sync.dma_start(tile[:], dram)
            return tile

        def entries(tile, cols):
            return tile[:, cols.start // 16 : cols.stop // 16]

        def load_scale_rows(rows, dram, queue):
            queue.dma_start(rows[0:P:8, :].bitcast(I32), dram[0].bitcast(I32))

        def place_scale_rows(plane, rows, queue, first):
            for r in range(first, 4):
                queue.dma_start(plane[r:P:32, :].bitcast(I32), rows[8 * r : P : 32, :].bitcast(I32))

        def deal_scales(dealt, raw):
            nc.gpsimd.tensor_copy(
                dealt.rearrange("p (t m) -> p t m", t=PACK), raw.rearrange("p (m t) -> p t m", t=PACK)
            )

        def gather_scales(name, window, offsets, queue):
            picked = sb(name + "_picked", [P, S], U8)
            plane = sb(name, [P, S], U8)
            nc.gpsimd.memset(plane[:].bitcast(I32), 0)
            nc.vector.tensor_copy(picked[:], window[:].indirect(offsets[:]))
            place_scale_rows(plane, picked, queue, 0)
            return plane

        def load_words(name, words, queue, on_scalar):
            raw = sb(name + "_raw_words", [P, 2 * H], U8)
            queue.dma_start(raw[:].bitcast(I32), words[0].bitcast(I32))
            dealt = sb(name + "_words", [P, 2 * H], U8)
            if on_scalar:
                nc.scalar.copy(
                    dealt[:].bitcast(U16).rearrange("p (t m) -> p t m", t=PACK),
                    raw[:].bitcast(U16).rearrange("p (m t) -> p t m", t=PACK),
                )
            else:
                nc.gpsimd.tensor_copy(
                    dealt[:].rearrange("p (t m b) -> p t m b", t=PACK, b=2),
                    raw[:].rearrange("p (m t b) -> p t m b", t=PACK, b=2),
                )
            return dealt

        def product(bank, weight, t, codes, scales, cols, start, stop):
            words, wscales = weight
            nc.tensor.matmul_mx(
                out=bank,
                lhsT=words[:, 2 * P * t : 2 * P * (t + 1)].bitcast(FP4X4),
                lhsT_scale=wscales[:, P * t : P * (t + 1)],
                rhs=codes[:, cols].bitcast(FP8X4),
                rhs_scale=scales[:, cols],
                start=start,
                stop=stop,
            )

        def rows_view(tile, cols):
            return tile[:, :, cols].rearrange("p t (c i) -> p c t i", i=4)

        def woven_view(tile, cols):
            return tile[:, PACK * cols.start : PACK * cols.stop].rearrange("p (c i t) -> p c t i", i=4, t=PACK)

        def quantize(codes, scales, woven, cols):
            nc.vector.quantize_mx(
                out=codes[:, cols].bitcast(FP8X4),
                scales=scales[:, cols],
                in_=woven[:, PACK * cols.start : PACK * cols.stop],
            )

        whole = slice(0, S)

        xw = sb("xw", [P, T], I32)
        xs_one = sb("xs_one", [P, T], U8)
        xs_runs = sb("xs_runs", [P, T], U8)
        first_raw = sb("first_raw", [P, H], U8)
        second_raw = sb("second_raw", [P, H], U8)
        later_raw = sb("later_raw", [P, 2 * H], U8)
        nc.vector.memset(xs_one[:].bitcast(I32), 0)
        nc.gpsimd.memset(first_raw[:].bitcast(I32), 0)
        offs_l = load_list("offs_l", offs)
        nc.sync.dma_start(xw[:], x_words[0].rearrange("p c r -> p (c r)").bitcast(I32))
        for r in range(4):
            nc.scalar.dma_start(xs_one[r:P:32, :].bitcast(I32), x_scales[0, r:16:4, :].bitcast(I32))
        w1_dealt = load_words("w1", w1_words, nc.sync, True)
        for r in range(4):
            queue = nc.sync if r < 2 else nc.gpsimd
            queue.dma_start(first_raw[r:P:32, :].bitcast(I32), w1_scales[0, r:16:4, :].bitcast(I32))
        warm = sb("warm", [P, 1], F32)
        nc.vector.memset(warm[:], 0.0)
        warm_out = sb("warm_out", [P, 1], F32)
        nc.scalar.activation(warm_out[:], warm[:], ACT.Sigmoid)

        nc.vector.memset(xs_runs[:].bitcast(I32), 0)
        nc.gpsimd.memset(second_raw[:].bitcast(I32), 0)
        nc.gpsimd.memset(later_raw[:].bitcast(I32), 0)
        first_scales = sb("first_scales", [P, H], U8)
        deal_scales(first_scales[:], first_raw[:])
        w1 = (w1_dealt, first_scales)

        qs = sb("qs", [P, S], U8)
        nc.vector.tensor_copy(qs[:], xs_one[:].indirect(offs_l[:]))
        qw = sb("qw", [P, S], U32)
        nc.vector.tensor_copy(qw[:], xw[:].bitcast(U32).indirect(offs_l[:]))
        y_ps = [psum.tile([P, S], F32, name="y_ps%d" % t, tag="a%d" % t) for t in range(PACK)]
        for t in range(PACK):
            product(y_ps[t][:], w1, t, qw, qs, whole, True, True)

        hz_l = load_list("hz_l", hz)
        load_scale_rows(xs_runs, x_scales, nc.sync)
        n1_l = load_list("n1_l", n1)
        n2_l = load_list("n2_l", n2)
        gm_sb = sb("gm_sb", [P, PACK], F32)
        nc.sync.dma_start(gm_sb[:], gm.rearrange("(p t) o -> p (t o)", t=PACK))
        gn_sb = sb("gn_sb", [P, PACK], F32)
        nc.sync.dma_start(gn_sb[:], gn.rearrange("(p t) o -> p (t o)", t=PACK))
        w2_dealt = load_words("w2", w2_words, nc.sync, False)
        for r in range(4):
            nc.sync.dma_start(second_raw[r:P:32, :].bitcast(I32), w2_scales[0, r:16:4, :].bitcast(I32))
        second_scales = sb("second_scales", [P, H], U8)
        deal_scales(second_scales[:], second_raw[:])
        w2 = (w2_dealt, second_scales)

        hs = gather_scales("hs", xs_runs, hz_l, nc.sync)
        hw = sb("hw", [P, S], U32)
        nc.vector.tensor_copy(hw[:], xw[:].bitcast(U32).indirect(hz_l[:]))
        d_ps = [psum.tile([P, S], F32, name="d_ps%d" % t, tag="b%d" % t) for t in range(PACK)]
        for t in range(PACK):
            product(d_ps[t][:], w2, t, hw, hs, whole, True, True)

        n3_l = load_list("n3_l", n3)
        n4_l = load_list("n4_l", n4)
        w3_dealt = load_words("w3", w3_words, nc.sync, False)
        w4_dealt = load_words("w4", w4_words, nc.sync, False)
        n5_l = load_list("n5_l", n5)
        later_scales = sb("later_scales", [P, 2 * H], U8)
        parts = [slice(H * i, H * (i + 1)) for i in range(2)]
        for part, dram in zip(parts, (w3_scales, w4_scales)):
            load_scale_rows(later_raw[:, part], dram, nc.sync)
            deal_scales(later_scales[:, part], later_raw[:, part])
        place_scale_rows(later_scales, later_scales, nc.sync, 1)
        w3 = (w3_dealt, later_scales[:, parts[0]])
        w4 = (w4_dealt, later_scales[:, parts[1]])

        gm_twice = sb("gm_twice", [P, PACK], F32)
        gm_sign = sb("gm_sign", [P, PACK], BF16)
        gm_size = sb("gm_size", [P, PACK], F32)
        nc.gpsimd.tensor_scalar(gm_twice[:], gm_sb[:], 0.0, 2.0, ALU.is_ge, ALU.mult)
        nc.gpsimd.tensor_scalar(gm_sign[:], gm_twice[:], 1.0, -1.0, ALU.mult, ALU.add)
        nc.gpsimd.tensor_tensor(gm_size[:], gm_sb[:], gm_sign[:], ALU.mult)

        y = [sb("y_win%d" % t, [P, S], F32) for t in range(PACK)]
        d = sb("d_win", [P, PACK, S], F32)
        y1 = [sb("y1_%d" % t, [P, S], F32) for t in range(PACK)]
        diff = [sb("diff%d" % t, [P, S], F32) for t in range(PACK)]
        gate = [sb("gate%d" % t, [P, S], F32) for t in range(PACK)]
        z_rows = sb("z_rows", [P, PACK, S], BF16)
        d3 = sb("d3", [P, PACK, S], F32)
        d4 = sb("d4", [P, PACK, S], F32)

        def fetch(on_vector, out, window, offsets):
            if on_vector:
                nc.vector.tensor_copy(out, window.indirect(offsets))
            else:
                nc.scalar.activation(out, window.indirect(offsets), ACT.Copy)

        def difference(t):
            if t in Y_ROWS_ON_VECTOR:
                nc.vector.tensor_copy(y[t][:], y_ps[t][:])
            else:
                nc.scalar.copy(y[t][:], y_ps[t][:])
            for cols in HALVES:
                fetch(t in Y1_ON_VECTOR, y1[t][:, cols], y[t][:], entries(n1_l, cols))
            for cols in HALVES:
                nc.vector.tensor_tensor(
                    diff[t][:, cols], y[t][:].indirect(entries(n2_l, cols)), y1[t][:, cols], ALU.subtract
                )

        def gated(t):
            nc.scalar.activation(gate[t][:], diff[t][:], ACT.Sigmoid, scale=-1.0)
            nc.vector.scalar_tensor_tensor(
                z_rows[:, t, :], y_ps[t][:], gn_sb[:, t : t + 1], gate[t][:], ALU.mult, ALU.mult
            )

        def d_rows(t):
            nc.scalar.activation(d[:, t, :], d_ps[t][:], ACT.Copy, scale=gm_size[:, t : t + 1])
            fetch(False, d3[:, t, CHUNKS[0]], d[:, t, :], entries(n3_l, CHUNKS[0]))

        for step in range(PACK + LAG):
            if step < PACK:
                difference(step)
            else:
                d_rows(step - PACK)
            if step >= LAG:
                gated(step - LAG)
        for t in range(LAG, PACK):
            d_rows(t)

        z_woven = sb("z_woven", [P, PACK * S], BF16)
        z_codes = sb("z_codes", [P, S], U32)
        z_scales = sb("z_scales", [P, S], U8)
        nc.vector.tensor_copy(woven_view(z_woven, whole), rows_view(z_rows, whole))
        for t in range(D4_ON_VECTOR):
            fetch(True, d4[:, t, CHUNKS[0]], d[:, t, :], entries(n4_l, CHUNKS[0]))
        quantize(z_codes, z_scales, z_woven, whole)

        h_ps = {}
        free_banks = ["b0", "b1", "b2", "b3", "a0", "a1"]
        for c, cols in enumerate(CHUNKS):
            width = cols.stop - cols.start
            for u in range(2):
                bank = psum.tile([P, 2, width], F32, name="h_ps%d_%d" % (c, u), tag=free_banks[2 * c + u])
                h_ps[c, u] = bank
                for e in range(2):
                    product(bank[:, e, :], w3, 2 * u + e, z_codes, z_scales, cols, e == 0, False)

        upper = sb("upper", [P, PACK, S], F32)
        z2_size = sb("z2_size", [P, PACK * S], BF16)
        z2_woven = sb("z2_woven", [P, PACK * S], BF16)
        z2_codes = sb("z2_codes", [P, S], U32)
        z2_scales = sb("z2_scales", [P, S], U8)
        h = [sb("h_win%d" % t, [P, S], F32) for t in range(PACK)]

        def h_rows(c):
            cols = CHUNKS[c]
            for t in range(PACK):
                if c == len(CHUNKS) - 1 and t >= 2:
                    nc.vector.tensor_copy(h[t][:, cols], h_ps[c, t // 2][:, t % 2, :])
                else:
                    nc.scalar.copy(h[t][:, cols], h_ps[c, t // 2][:, t % 2, :])

        for c, cols in enumerate(CHUNKS):
            width = cols.stop - cols.start
            if c > 0:
                for t in range(PACK):
                    fetch(False, d3[:, t, cols], d[:, t, :], entries(n3_l, cols))
            nc.vector.tensor_tensor(upper[:, :, cols], d[:, :, cols], d3[:, :, cols], ALU.max)
            for t in range(D4_ON_VECTOR if c == 0 else 0, PACK):
                fetch(False, d4[:, t, cols], d[:, t, :], entries(n4_l, cols))
            nc.vector.tensor_tensor(woven_view(z2_size, cols), rows_view(upper, cols), rows_view(d4, cols), ALU.min)
            span = slice(PACK * cols.start, PACK * cols.stop)
            nc.vector.tensor_tensor(
                z2_woven[:, span].rearrange("p (j t) -> p j t", t=PACK),
                z2_size[:, span].rearrange("p (j t) -> p j t", t=PACK),
                gm_sign[:].unsqueeze(1).broadcast_to([P, width, PACK]),
                ALU.mult,
            )
            quantize(z2_codes, z2_scales, z2_woven, cols)
            for t in range(PACK):
                product(h_ps[c, t // 2][:, t % 2, :], w4, t, z2_codes, z2_scales, cols, False, t % 2 == 1)
        for c in range(len(CHUNKS)):
            h_rows(c)

        h5 = sb("h5", [P, PACK, S], F32)
        res = sb("res", [P, PACK, S], F32)
        res_woven = sb("res_woven", [P, PACK * S], BF16)
        res_codes = sb("res_codes", [P, S], I32)
        res_scales = sb("res_scales", [P, S], U8)
        out_rows = out_0.rearrange("(p t) j -> p t j", t=PACK)
        out_words = out_1[0].rearrange("p c r -> p (c r)").bitcast(I32)
        for c, cols in enumerate(CHUNKS):
            for t in range(PACK):
                fetch(c == 0 and t in H5_ON_VECTOR, h5[:, t, cols], h[t][:], entries(n5_l, cols))
            for u in range(2):
                pair = slice(2 * u, 2 * u + 2)
                nc.vector.tensor_tensor(res[:, pair, cols], h_ps[c, u][:], h5[:, pair, cols], ALU.subtract)
            nc.sync.dma_start(out_rows[:, :, cols], res[:, :, cols])
            nc.vector.tensor_copy(woven_view(res_woven, cols), rows_view(res, cols))
            quantize(res_codes, res_scales, res_woven, cols)
            nc.sync.dma_start(out_words[:, cols], res_codes[:, cols])
        for r in range(4):
            queue = nc.scalar if r % 2 else nc.sync
            queue.dma_start(out_2[0, r:16:4, :].bitcast(I32), res_scales[r:P:32, :].bitcast(I32))
